import numpy as np
import ml_dtypes


def mxq(x, axis, fmt="e4m3"):
    dtype, down = {"e4m3": (ml_dtypes.float8_e4m3fn, 7), "e5m2": (ml_dtypes.float8_e5m2, 14)}[fmt]
    v = np.moveaxis(np.asarray(x, np.float32).astype(ml_dtypes.bfloat16).astype(np.float64), axis, -1)
    blocks = v.reshape(v.shape[:-1] + (-1, 32))
    amax = np.abs(blocks).max(-1, keepdims=True)
    byte = np.maximum(np.where(amax > 0, np.frexp(amax)[1] - 1 + 127, 0) - down, 1)
    scale = np.exp2(byte - 127.0)
    codes = (blocks / scale).astype(np.float32).astype(dtype).astype(np.float64)
    return np.moveaxis((codes * scale).reshape(v.shape), -1, axis)


WIDE = False


def mx_kscale(k):
    if not WIDE:
        return np.ones(k)
    levels = np.array([10, -10, 5, -5, 0])
    if k % 512:
        return np.exp2(np.random.permutation(np.resize(levels, k // 32))).repeat(32)
    a = np.empty((k // 512, 16))
    for p in range(k // 512):
        a[p, :8] = np.random.permutation(np.resize(levels, 8))
        for g in range(8):
            far = levels[np.abs(levels - a[p, g]) >= 10]
            a[p, g + 8] = far[np.random.randint(len(far))]
    return np.exp2(a.ravel()).repeat(32)


BF16 = ml_dtypes.bfloat16


def bf(x):
    return np.asarray(x, np.float32).astype(BF16)


def f64(x):
    return np.asarray(x).astype(np.float64)


E2M1 = np.array([0.0, 0.5, 1.0, 1.5, 2.0, 3.0, 4.0, 6.0, -0.0, -0.5, -1.0, -1.5, -2.0, -3.0, -4.0, -6.0])


def pack_weight(w, fmt):
    k, n = w.shape
    w = f64(bf(w)).reshape(k // 32, 32, n)
    amax = np.abs(w).max(1)
    if fmt == "e4m3":
        byte = np.frexp(amax)[1] - 1 + 127 - 7
    else:
        mant, ex = np.frexp(amax / 6.0)
        byte = np.where(mant > 0.5, ex, ex - 1) + 127
    byte = np.clip(np.where(amax > 0, byte, 1), 1, 254)
    scaled = (w * np.exp2(127.0 - byte)[:, None, :]).reshape(k, n).astype(np.float32)
    by_word = np.ascontiguousarray(scaled.reshape(k // 512, 128, 4, n).transpose(0, 1, 3, 2))
    if fmt == "e4m3":
        words = by_word.astype(ml_dtypes.float8_e4m3fn).view(np.uint8)
    else:
        c = by_word.astype(ml_dtypes.float4_e2m1fn).view(np.uint8) & 0xF
        words = c[..., 0::2] | (c[..., 1::2] << 4)
    return np.ascontiguousarray(words), np.ascontiguousarray(byte.astype(np.uint8).reshape(k // 512, 16, n))


def unpack_weight(words, scales, fmt):
    g, p, n, _ = words.shape
    if fmt == "e4m3":
        vals = np.ascontiguousarray(words).view(ml_dtypes.float8_e4m3fn).astype(np.float64)
    else:
        nib = np.empty((g, p, n, 4), np.uint8)
        nib[..., 0::2] = words & 0xF
        nib[..., 1::2] = words >> 4
        vals = E2M1[nib]
    vals = vals * np.repeat(np.exp2(scales.astype(np.float64) - 127.0), 8, axis=1)[..., None]
    return vals.transpose(0, 1, 3, 2).reshape(g * 512, n)
def pack4(w):
    words, scales = pack_weight(w, "e2m1")
    return words.reshape(words.shape[0], 128, -1), scales


def unpack4(words, scales):
    return unpack_weight(words.reshape(words.shape[0], 128, -1, 2), scales, "e2m1")


def planes(Y):
    n, m = Y.shape
    b = f64(bf(Y)).reshape(n // 32, 32, m)
    amax = np.abs(b).max(1)
    byte = np.clip(np.where(amax > 0, np.frexp(amax)[1] - 1 + 127 - 7, 1), 1, 254)
    codes = (b * np.exp2(127.0 - byte)[:, None, :]).reshape(n, m).astype(np.float32).astype(ml_dtypes.float8_e4m3fn).view(np.uint8)
    words = codes.reshape(n // 512, 128, 4, m).transpose(0, 1, 3, 2)
    return np.ascontiguousarray(words), np.ascontiguousarray(byte.astype(np.uint8).reshape(n // 512, 16, m))


H, LQ, LK, D, UNIT = 8, 256, 1536, 1024, 512

LENGTH = LK / UNIT


def setup_inputs():
    s = mx_kscale(D)
    x = np.random.randn(D, H * LQ) * s[:, None]
    x_words, x_scales = pack_weight(f64(bf(x)), "e4m3")
    keys = bf(np.random.randn(LK, D) / np.sqrt(D) / s[None, :])
    rel_table = bf(1.2 + 0.5 * np.random.randn(H, LQ + LK - 1))
    key_gain = bf(np.exp(0.8 * np.random.randn(LK)))
    return {"x_words": x_words, "x_scales": x_scales, "keys": keys,
            "rel_table": rel_table, "key_gain": key_gain}


def reference(x_words, x_scales, keys, rel_table, key_gain):
    x = unpack_weight(x_words, x_scales, "e4m3")
    kq = mxq(f64(keys), 1, "e4m3")
    scores = (x.T @ kq.T).reshape(H, LQ, LK)
    offset = np.arange(LK)[None, :] - np.arange(LQ)[:, None] + LQ - 1
    bias = f64(rel_table)[:, offset]
    y = np.maximum(scores + bias, 0.0) * f64(key_gain)[None, None, :] / LENGTH
    Y = y.reshape(H * LQ, LK).T
    words, scales = planes(Y)
    return y, words, scales

@@ -1,0 +1,273 @@
+from contextlib import ExitStack
+
+import concourse.mybir as mybir
+from concourse.masks import make_identity
+
+H, LQ, LK, D = 8, 256, 1536, 1024
+TOKENS = H * LQ
+FLOPS = 2 * TOKENS * LK * D
+
+F32 = mybir.dt.float32
+BF16 = mybir.dt.bfloat16
+I32 = mybir.dt.int32
+U32 = mybir.dt.uint32
+U8 = mybir.dt.uint8
+FP8X4 = mybir.dt.float8_e4m3fn_x4
+ALU = mybir.AluOpType
+
+P = 128
+PACK = 4
+GROUP = P * PACK
+GROUPS = LK // GROUP
+PASSES = D // GROUP
+CHUNK = 512
+CHUNKS = TOKENS // CHUNK
+UNITS = GROUPS * CHUNKS
+SUBS = CHUNK // P
+CAST_ON_VECTOR = 160
+
+ROW_LEN = 720
+ROW_WORDS = ROW_LEN // 2
+SORT_LEN = 132
+HEAD_WORDS = 132
+
+
+def tile_relu_relative_scores_g6_kernel(tc, x_words, x_scales, keys, rel_table, key_gain, out_0, out_1, out_2):
+    nc = tc.nc
+    y_rows = out_0.rearrange("h i j -> (h i) j")
+
+    with ExitStack() as ctx:
+        keep = ctx.enter_context(tc.tile_pool(name="keep", bufs=1))
+        work = ctx.enter_context(tc.tile_pool(name="work", bufs=3))
+        psum = ctx.enter_context(tc.psum_pool(name="psum", bufs=1))
+        ctx.enter_context(tc.manual_schedule())
+
+        turn_count = []
+
+        def turn_bank():
+            bank = psum.tile([P, PACK, P], F32, name="turn", tag="turn%d" % (len(turn_count) % 4))
+            turn_count.append(0)
+            return bank
+
+        ident = keep.tile([P, P], F32)
+        x_scale = keep.tile([P, TOKENS], U8, align_bytes=64)
+        gain_raw = keep.tile([P, GROUPS, PACK], BF16)
+        gain = keep.tile([P, GROUPS, PACK], F32)
+        rel_rows = [keep.tile([P, ROW_LEN], BF16, name="rel_rows%d" % g) for g in range(GROUPS)]
+        bias = [keep.tile([P, H, HEAD_WORDS], F32, name="bias%d" % g) for g in range(GROUPS)]
+        x_codes = [keep.tile([P, PASSES, CHUNK], U32, name="x_codes%d" % c, align_bytes=64) for c in range(CHUNKS)]
+        key_raw = {}
+        key_codes = {}
+        key_scale = {}
+        for g in range(GROUPS):
+            for half in range(2):
+                key_raw[g, half] = keep.tile([P, 2 * D], BF16, name="key_raw%d%d" % (g, half))
+                key_codes[g, half] = keep.tile([P, 2 * PASSES * P], U32, name="key_codes%d%d" % (g, half), align_bytes=64)
+                key_scale[g, half] = keep.tile([P, 2 * PASSES * P], U8, name="key_scale%d%d" % (g, half), align_bytes=64)
+        y_scale = [keep.tile([P, TOKENS], U8, name="y_scale%d" % g, align_bytes=64) for g in range(GROUPS)]
+
+        def load_rel(g):
+            for r in range(4):
+                first = GROUP * g + 16 * r
+                width = min(ROW_LEN, LQ + LK - 1 - first)
+                nc.sync.dma_start(
+                    out=rel_rows[g][r:P:4, 0:width],
+                    in_=rel_table[:, first : first + width].unsqueeze(0).broadcast_to([4, H, width]),
+                )
+
+        def load_keys(g, half):
+            rows = keys[GROUP * g : GROUP * (g + 1), :].rearrange("(m t) k -> m (t k)", t=PACK)
+            nc.sync.dma_start(out=key_raw[g, half][:], in_=rows[:, 2 * D * half : 2 * D * (half + 1)])
+
+        def load_x(c):
+            src = x_words[:, :, CHUNK * c : CHUNK * (c + 1), :].rearrange("g p n t -> p g (n t)")
+            nc.sync.dma_start(out=x_codes[c][:].bitcast(I32), in_=src.bitcast(I32))
+
+        def sort_rel(g):
+            rel_sorted = work.tile([P, 2, SORT_LEN], F32, name="rel_sorted", bufs=2)
+            words = rel_rows[g][:].bitcast(F32)
+            for q in range(4):
+                rows = slice(32 * q, 32 * (q + 1))
+                nc.vector.tensor_copy(
+                    out=rel_sorted[rows, :, :],
+                    in_=words[rows, 32 * q : 32 * q + 2 * SORT_LEN].rearrange("p (m u) -> p u m", u=2),
+                )
+            return rel_sorted
+
+        def turn_rel(g, rel_sorted, second_copy):
+            for b in range(3):
+                bank = turn_bank()
+                count = 4 if b < 2 else 2
+                for w in range(count):
+                    word = 4 * b + w
+                    nc.tensor.transpose(bank[:, w, :], rel_sorted[:, word % 2, word // 2 : word // 2 + P], ident[:])
+                if b < 2:
+                    dst = bias[g][:, :, 0:P].rearrange("p h (q r w) -> p q h r w", q=4, r=4)[:, :, :, :, 4 * b : 4 * b + 4]
+                    src = bank[:].rearrange("p w (q h r) -> p q h r w", q=4, r=4)
+                    copy = nc.scalar.copy if b == 0 else second_copy
+                    copy(out=dst, in_=src)
+                else:
+                    nc.scalar.copy(out=bias[g][:, :, P : P + 2], in_=bank[:, 0:2, 99:P:4].rearrange("p w h -> p h w"))
+
+        def turn_keys(g, half, second_copy):
+            grouped = work.tile([P, 2, PASSES, P, 2], F32, name="grouped", bufs=2, align_bytes=64)
+            words = key_raw[g, half][:].bitcast(F32)
+            for slot in range(2):
+                bank = turn_bank()
+                for k in range(PASSES):
+                    for u in range(2):
+                        first = 512 * slot + 256 * k
+                        nc.tensor.transpose(bank[:, 2 * k + u, :], words[:, first + u : first + 256 : 2], ident[:])
+                copy = nc.scalar.copy if slot == 0 else second_copy
+                copy(out=grouped[:, slot], in_=bank[:].rearrange("p (k u) m -> p k m u", u=2))
+            return grouped
+
+        def quantize_keys(g, half, grouped):
+            nc.vector.quantize_mx(
+                out=key_codes[g, half][:].bitcast(FP8X4),
+                scales=key_scale[g, half][:],
+                in_=grouped[:].rearrange("p s k m u -> p (s k m u)").bitcast(BF16),
+            )
+
+        def scores(n, t):
+            g, c = divmod(n, CHUNKS)
+            bank = psum.tile([P, CHUNK], F32, name="score", tag="score%d" % t)
+            for k in range(PASSES):
+                cols = slice(P * (PASSES * (t % 2) + k), P * (PASSES * (t % 2) + k + 1))
+                nc.tensor.matmul_mx(
+                    out=bank[:],
+                    lhsT=key_codes[g, t // 2][:, cols].bitcast(FP8X4),
+                    lhsT_scale=key_scale[g, t // 2][:, cols],
+                    rhs=x_codes[c][:, k, :].bitcast(FP8X4),
+                    rhs_scale=x_scale[4 * k : P, CHUNK * c : CHUNK * (c + 1)],
+                    start=(k == 0),
+                    stop=(k == PASSES - 1),
+                )
+            return bank
+
+        def add_bias(n, t, bank, y_t):
+            g, c = divmod(n, CHUNKS)
+            window = bias[g][:].bitcast(BF16)[:, 2 * c : 2 * c + 2, t : t + LQ]
+            nc.vector.tensor_tensor(
+                out=y_t[:, t, :].rearrange("p (h i) -> p h i", h=2),
+                in0=bank[:].rearrange("p (h i) -> p h i", h=2),
+                in1=window[:, :, ::-1],
+                op=ALU.add,
+            )
+
+        def relu_gain(n, t, y_t):
+            g = n // CHUNKS
+            nc.vector.tensor_scalar(
+                out=y_t[:, t, :], in0=y_t[:, t, :], scalar1=0.0, scalar2=gain[:, g, t : t + 1], op0=ALU.max, op1=ALU.mult
+            )
+
+        def round_part(copy, y_t, y_bf, first, last):
+            copy(
+                out=y_bf[:, first:last, :].rearrange("p (c i) t -> p c t i", i=4),
+                in_=y_t[:, :, first:last].rearrange("p t (c i) -> p c t i", i=4),
+            )
+
+        def quantize_y(n, y_bf):
+            g, c = divmod(n, CHUNKS)
+            y_codes = work.tile([P, CHUNK], U32, name="y_codes", align_bytes=64)
+            nc.vector.quantize_mx(
+                out=y_codes[:].bitcast(FP8X4),
+                scales=y_scale[g][:, CHUNK * c : CHUNK * (c + 1)],
+                in_=y_bf[:].rearrange("p n t -> p (n t)"),
+            )
+            dst = out_1[g, :, CHUNK * c : CHUNK * (c + 1), :].rearrange("p n t -> p (n t)")
+            nc.sync.dma_start(out=dst.bitcast(I32), in_=y_codes[:].bitcast(I32))
+            if c == CHUNKS - 1:
+                for q in range(4):
+                    nc.sync.dma_start(
+                        out=out_2[g, 4 * q : 4 * q + 4, :].bitcast(I32),
+                        in_=y_scale[g][32 * q : 32 * q + 4, :].bitcast(I32),
+                    )
+
+        def turn_y(y_t):
+            banks = []
+            for s in range(SUBS):
+                bank = turn_bank()
+                for t in range(PACK):
+                    nc.tensor.transpose(bank[:, t, :], y_t[:, t, P * s : P * (s + 1)], ident[:])
+                banks.append(bank)
+            return banks
+
+        def store_y(n, banks, per_store):
+            g, c = divmod(n, CHUNKS)
+            for first in range(0, SUBS, per_store):
+                y_out = work.tile([P, per_store, P, PACK], F32, name="y_out", tag="y_out", bufs=4)
+                for s in range(per_store):
+                    nc.scalar.copy(out=y_out[:, s], in_=banks[first + s][:].rearrange("q t p -> q p t"))
+                row = CHUNK * c + P * first
+                dst = y_rows[row : row + P * per_store, GROUP * g : GROUP * (g + 1)]
+                nc.sync.dma_start(
+                    out=dst.rearrange("(s q) j -> q s j", q=P),
+                    in_=y_out[:].rearrange("q s p t -> q s (p t)"),
+                )
+
+        nc.vector.memset(x_scale[:].bitcast(U32), 0)
+        nc.vector.memset(rel_rows[GROUPS - 1][:, ROW_LEN - 2 : ROW_LEN], 0.0)
+        make_identity(nc, ident[:])
+        load_rel(0)
+        load_keys(0, 0)
+        load_keys(0, 1)
+        load_x(0)
+        nc.sync.dma_start(out=gain_raw[:], in_=key_gain.rearrange("(g p t) -> p g t", p=P, t=PACK))
+        for q in range(4):
+            nc.sync.dma_start(
+                out=x_scale[32 * q : 32 * q + 4 * PASSES, :].bitcast(I32),
+                in_=x_scales[:, 4 * q : 4 * q + 4, :].bitcast(I32),
+            )
+        load_x(1)
+        load_keys(1, 0)
+        load_x(2)
+        load_keys(1, 1)
+        load_rel(1)
+        load_x(3)
+        load_keys(2, 0)
+        load_keys(2, 1)
+        load_rel(2)
+
+        turn_rel(0, sort_rel(0), nc.vector.tensor_copy)
+        nc.vector.tensor_scalar(out=gain[:], in0=gain_raw[:], scalar1=1.0 / GROUPS, scalar2=None, op0=ALU.mult)
+        grouped_first = turn_keys(0, 0, nc.vector.tensor_copy)
+        grouped_second = turn_keys(0, 1, nc.scalar.copy)
+        quantize_keys(0, 0, grouped_first)
+        quantize_keys(0, 1, grouped_second)
+        score = [scores(0, t) for t in range(PACK)]
+
+        before = None
+        waiting_keys = None
+        rel_sorted = None
+        for n in range(UNITS):
+            g, c = divmod(n, CHUNKS)
+            prepare = g + 1 < GROUPS
+            y_t = work.tile([P, PACK, CHUNK], F32, name="y_t")
+            for t in range(PACK):
+                add_bias(n, t, score[t], y_t)
+                if n + 1 < UNITS:
+                    score[t] = scores(n + 1, t)
+                if t == 0 and before is not None:
+                    round_part(nc.vector.tensor_copy, before[0], before[1], CHUNK - CAST_ON_VECTOR, CHUNK)
+                if t > 0:
+                    relu_gain(n, t - 1, y_t)
+                if t == 1 and waiting_keys is not None:
+                    quantize_keys(*waiting_keys)
+                    waiting_keys = None
+            relu_gain(n, PACK - 1, y_t)
+            if before is not None:
+                quantize_y(n - 1, before[1])
+            y_bf = work.tile([P, CHUNK, PACK], BF16, name="y_bf", align_bytes=64)
+            if n + 1 < UNITS:
+                round_part(nc.scalar.copy, y_t, y_bf, 0, CHUNK - CAST_ON_VECTOR)
+            if prepare and c < 2:
+                waiting_keys = (g + 1, c, turn_keys(g + 1, c, nc.scalar.copy))
+            if prepare and c == 1:
+                rel_sorted = sort_rel(g + 1)
+            if prepare and c == 2:
+                turn_rel(g + 1, rel_sorted, nc.scalar.copy)
+            store_y(n, turn_y(y_t), 2 if n + 1 < UNITS else 1)
+            before = (y_t, y_bf)
+        round_part(nc.vector.tensor_copy, before[0], before[1], 0, CHUNK)
+        quantize_y(UNITS - 1, before[1])

@@ -24,7 +24,12 @@ CHUNK = 512
 CHUNKS = TOKENS // CHUNK
 UNITS = GROUPS * CHUNKS
 SUBS = CHUNK // P
-CAST_ON_VECTOR = 160
+CAST_ON_VECTOR_PREPARING = 176
+CAST_ON_VECTOR_LAST = 96
+SLOTS = GROUPS * PACK
+SCORE_BANKS = 3
+TURN_BANKS = 5
+LENGTH = LK / 512
 
 ROW_LEN = 720
 ROW_WORDS = ROW_LEN // 2
@@ -45,7 +50,7 @@ def tile_relu_relative_scores_g6_kernel(tc, x_words, x_scales, keys, rel_table, 
         turn_count = []
 
         def turn_bank():
-            bank = psum.tile([P, PACK, P], F32, name="turn", tag="turn%d" % (len(turn_count) % 4))
+            bank = psum.tile([P, PACK, P], F32, name="turn", tag="turn%d" % (len(turn_count) % TURN_BANKS))
             turn_count.append(0)
             return bank
 
@@ -56,14 +61,9 @@ def tile_relu_relative_scores_g6_kernel(tc, x_words, x_scales, keys, rel_table, 
         rel_rows = [keep.tile([P, ROW_LEN], BF16, name="rel_rows%d" % g) for g in range(GROUPS)]
         bias = [keep.tile([P, H, HEAD_WORDS], F32, name="bias%d" % g) for g in range(GROUPS)]
         x_codes = [keep.tile([P, PASSES, CHUNK], U32, name="x_codes%d" % c, align_bytes=64) for c in range(CHUNKS)]
-        key_raw = {}
-        key_codes = {}
-        key_scale = {}
-        for g in range(GROUPS):
-            for half in range(2):
-                key_raw[g, half] = keep.tile([P, 2 * D], BF16, name="key_raw%d%d" % (g, half))
-                key_codes[g, half] = keep.tile([P, 2 * PASSES * P], U32, name="key_codes%d%d" % (g, half), align_bytes=64)
-                key_scale[g, half] = keep.tile([P, 2 * PASSES * P], U8, name="key_scale%d%d" % (g, half), align_bytes=64)
+        key_raw = [keep.tile([P, D], BF16, name="key_raw%d" % s) for s in range(SLOTS)]
+        key_codes = [keep.tile([P, PASSES * P], U32, name="key_codes%d" % s, align_bytes=64) for s in range(SLOTS)]
+        key_scale = [keep.tile([P, PASSES * P], U8, name="key_scale%d" % s, align_bytes=64) for s in range(SLOTS)]
         y_scale = [keep.tile([P, TOKENS], U8, name="y_scale%d" % g, align_bytes=64) for g in range(GROUPS)]
 
         def load_rel(g):
@@ -75,9 +75,9 @@ def tile_relu_relative_scores_g6_kernel(tc, x_words, x_scales, keys, rel_table, 
                     in_=rel_table[:, first : first + width].unsqueeze(0).broadcast_to([4, H, width]),
                 )
 
-        def load_keys(g, half):
-            rows = keys[GROUP * g : GROUP * (g + 1), :].rearrange("(m t) k -> m (t k)", t=PACK)
-            nc.sync.dma_start(out=key_raw[g, half][:], in_=rows[:, 2 * D * half : 2 * D * (half + 1)])
+        def load_keys(slot):
+            g, t = divmod(slot, PACK)
+            nc.sync.dma_start(out=key_raw[slot][:], in_=keys[GROUP * g + t : GROUP * (g + 1) : PACK, :])
 
         def load_x(c):
             src = x_words[:, :, CHUNK * c : CHUNK * (c + 1), :].rearrange("g p n t -> p g (n t)")
@@ -94,56 +94,54 @@ def tile_relu_relative_scores_g6_kernel(tc, x_words, x_scales, keys, rel_table, 
                 )
             return rel_sorted
 
-        def turn_rel(g, rel_sorted, second_copy):
-            for b in range(3):
-                bank = turn_bank()
-                count = 4 if b < 2 else 2
-                for w in range(count):
-                    word = 4 * b + w
-                    nc.tensor.transpose(bank[:, w, :], rel_sorted[:, word % 2, word // 2 : word // 2 + P], ident[:])
-                if b < 2:
-                    dst = bias[g][:, :, 0:P].rearrange("p h (q r w) -> p q h r w", q=4, r=4)[:, :, :, :, 4 * b : 4 * b + 4]
-                    src = bank[:].rearrange("p w (q h r) -> p q h r w", q=4, r=4)
-                    copy = nc.scalar.copy if b == 0 else second_copy
-                    copy(out=dst, in_=src)
-                else:
-                    nc.scalar.copy(out=bias[g][:, :, P : P + 2], in_=bank[:, 0:2, 99:P:4].rearrange("p w h -> p h w"))
+        def turn_rel(g, rel_sorted, b, copy):
+            bank = turn_bank()
+            count = 4 if b < 2 else 2
+            for w in range(count):
+                word = 4 * b + w
+                nc.tensor.transpose(bank[:, w, :], rel_sorted[:, word % 2, word // 2 : word // 2 + P], ident[:])
+            if b < 2:
+                dst = bias[g][:, :, 0:P].rearrange("p h (q r w) -> p q h r w", q=4, r=4)[:, :, :, :, 4 * b : 4 * b + 4]
+                copy(out=dst, in_=bank[:].rearrange("p w (q h r) -> p q h r w", q=4, r=4))
+            else:
+                copy(out=bias[g][:, :, P : P + 2], in_=bank[:, 0:2, 99:P:4].rearrange("p w h -> p h w"))
 
-        def turn_keys(g, half, second_copy):
-            grouped = work.tile([P, 2, PASSES, P, 2], F32, name="grouped", bufs=2, align_bytes=64)
-            words = key_raw[g, half][:].bitcast(F32)
-            for slot in range(2):
-                bank = turn_bank()
-                for k in range(PASSES):
-                    for u in range(2):
-                        first = 512 * slot + 256 * k
-                        nc.tensor.transpose(bank[:, 2 * k + u, :], words[:, first + u : first + 256 : 2], ident[:])
-                copy = nc.scalar.copy if slot == 0 else second_copy
-                copy(out=grouped[:, slot], in_=bank[:].rearrange("p (k u) m -> p k m u", u=2))
+        def turn_keys(slot):
+            grouped = work.tile([P, PASSES, P, 2], F32, name="grouped", bufs=4, align_bytes=64)
+            words = key_raw[slot][:].bitcast(F32)
+            bank = turn_bank()
+            for k in range(PASSES):
+                for u in range(2):
+                    nc.tensor.transpose(bank[:, 2 * k + u, :], words[:, 256 * k + u : 256 * (k + 1) : 2], ident[:])
+            nc.scalar.copy(out=grouped[:], in_=bank[:].rearrange("p (k u) m -> p k m u", u=2))
             return grouped
 
-        def quantize_keys(g, half, grouped):
+        def quantize_keys(slot, grouped):
             nc.vector.quantize_mx(
-                out=key_codes[g, half][:].bitcast(FP8X4),
-                scales=key_scale[g, half][:],
-                in_=grouped[:].rearrange("p s k m u -> p (s k m u)").bitcast(BF16),
+                out=key_codes[slot][:].bitcast(FP8X4),
+                scales=key_scale[slot][:],
+                in_=grouped[:].rearrange("p k m u -> p (k m u)").bitcast(BF16),
             )
 
-        def scores(n, t):
-            g, c = divmod(n, CHUNKS)
-            bank = psum.tile([P, CHUNK], F32, name="score", tag="score%d" % t)
-            for k in range(PASSES):
-                cols = slice(P * (PASSES * (t % 2) + k), P * (PASSES * (t % 2) + k + 1))
-                nc.tensor.matmul_mx(
-                    out=bank[:],
-                    lhsT=key_codes[g, t // 2][:, cols].bitcast(FP8X4),
-                    lhsT_scale=key_scale[g, t // 2][:, cols],
-                    rhs=x_codes[c][:, k, :].bitcast(FP8X4),
-                    rhs_scale=x_scale[4 * k : P, CHUNK * c : CHUNK * (c + 1)],
-                    start=(k == 0),
-                    stop=(k == PASSES - 1),
-                )
-            return bank
+        score = []
+
+        def scores_up_to(last):
+            for index in range(len(score), min(last + 1, UNITS * PACK)):
+                n, t = divmod(index, PACK)
+                g, c = divmod(n, CHUNKS)
+                slot = PACK * g + t
+                bank = psum.tile([P, CHUNK], F32, name="score", tag="score%d" % (index % SCORE_BANKS))
+                for k in range(PASSES):
+                    nc.tensor.matmul_mx(
+                        out=bank[:],
+                        lhsT=key_codes[slot][:, P * k : P * (k + 1)].bitcast(FP8X4),
+                        lhsT_scale=key_scale[slot][:, P * k : P * (k + 1)],
+                        rhs=x_codes[c][:, k, :].bitcast(FP8X4),
+                        rhs_scale=x_scale[4 * k : P, CHUNK * c : CHUNK * (c + 1)],
+                        start=(k == 0),
+                        stop=(k == PASSES - 1),
+                    )
+                score.append(bank)
 
         def add_bias(n, t, bank, y_t):
             g, c = divmod(n, CHUNKS)
@@ -184,90 +182,103 @@ def tile_relu_relative_scores_g6_kernel(tc, x_words, x_scales, keys, rel_table, 
                         in_=y_scale[g][32 * q : 32 * q + 4, :].bitcast(I32),
                     )
 
-        def turn_y(y_t):
-            banks = []
-            for s in range(SUBS):
+        def store_y(n, y_t, first, count):
+            g, c = divmod(n, CHUNKS)
+            y_out = work.tile([P, count, P, PACK], F32, name="y_out", tag="y_out", bufs=4)
+            for s in range(count):
                 bank = turn_bank()
                 for t in range(PACK):
-                    nc.tensor.transpose(bank[:, t, :], y_t[:, t, P * s : P * (s + 1)], ident[:])
-                banks.append(bank)
-            return banks
+                    nc.tensor.transpose(bank[:, t, :], y_t[:, t, P * (first + s) : P * (first + s + 1)], ident[:])
+                nc.scalar.copy(out=y_out[:, s], in_=bank[:].rearrange("q t p -> q p t"))
+            row = CHUNK * c + P * first
+            dst = y_rows[row : row + P * count, GROUP * g : GROUP * (g + 1)]
+            nc.sync.dma_start(
+                out=dst.rearrange("(s q) j -> q s j", q=P),
+                in_=y_out[:].rearrange("q s p t -> q s (p t)"),
+            )
 
-        def store_y(n, banks, per_store):
-            g, c = divmod(n, CHUNKS)
-            for first in range(0, SUBS, per_store):
-                y_out = work.tile([P, per_store, P, PACK], F32, name="y_out", tag="y_out", bufs=4)
-                for s in range(per_store):
-                    nc.scalar.copy(out=y_out[:, s], in_=banks[first + s][:].rearrange("q t p -> q p t"))
-                row = CHUNK * c + P * first
-                dst = y_rows[row : row + P * per_store, GROUP * g : GROUP * (g + 1)]
-                nc.sync.dma_start(
-                    out=dst.rearrange("(s q) j -> q s j", q=P),
-                    in_=y_out[:].rearrange("q s p t -> q s (p t)"),
-                )
-
-        nc.vector.memset(x_scale[:].bitcast(U32), 0)
-        nc.vector.memset(rel_rows[GROUPS - 1][:, ROW_LEN - 2 : ROW_LEN], 0.0)
-        make_identity(nc, ident[:])
-        load_rel(0)
-        load_keys(0, 0)
-        load_keys(0, 1)
-        load_x(0)
-        nc.sync.dma_start(out=gain_raw[:], in_=key_gain.rearrange("(g p t) -> p g t", p=P, t=PACK))
-        for q in range(4):
+        def load_x_scale(q):
             nc.sync.dma_start(
                 out=x_scale[32 * q : 32 * q + 4 * PASSES, :].bitcast(I32),
                 in_=x_scales[:, 4 * q : 4 * q + 4, :].bitcast(I32),
             )
+
+        nc.vector.memset(x_scale[:].bitcast(U32), 0)
+        nc.vector.memset(rel_rows[GROUPS - 1][:, ROW_LEN - 2 : ROW_LEN], 0.0)
+        make_identity(nc, ident[:])
+        load_keys(0)
+        load_rel(0)
+        load_x(0)
+        for q in range(4):
+            load_x_scale(q)
+        for slot in range(1, PACK):
+            load_keys(slot)
+        nc.sync.dma_start(out=gain_raw[:], in_=key_gain.rearrange("(g p t) -> p g t", p=P, t=PACK))
+        load_keys(4)
         load_x(1)
-        load_keys(1, 0)
-        load_x(2)
-        load_keys(1, 1)
+        load_keys(5)
         load_rel(1)
+        load_keys(6)
+        load_x(2)
+        load_keys(7)
         load_x(3)
-        load_keys(2, 0)
-        load_keys(2, 1)
+        for slot in range(2 * PACK, SLOTS):
+            load_keys(slot)
         load_rel(2)
 
-        turn_rel(0, sort_rel(0), nc.vector.tensor_copy)
-        nc.vector.tensor_scalar(out=gain[:], in0=gain_raw[:], scalar1=1.0 / GROUPS, scalar2=None, op0=ALU.mult)
-        grouped_first = turn_keys(0, 0, nc.vector.tensor_copy)
-        grouped_second = turn_keys(0, 1, nc.scalar.copy)
-        quantize_keys(0, 0, grouped_first)
-        quantize_keys(0, 1, grouped_second)
-        score = [scores(0, t) for t in range(PACK)]
+        rel_sorted = sort_rel(0)
+        grouped = turn_keys(0)
+        turn_rel(0, rel_sorted, 0, nc.scalar.copy)
+        quantize_keys(0, grouped)
+        turn_rel(0, rel_sorted, 1, nc.vector.tensor_copy)
+        turn_rel(0, rel_sorted, 2, nc.vector.tensor_copy)
+        grouped = turn_keys(1)
+        scores_up_to(0)
+        nc.vector.tensor_scalar(out=gain[:], in0=gain_raw[:], scalar1=1.0 / LENGTH, scalar2=None, op0=ALU.mult)
+        quantize_keys(1, grouped)
+        waiting = [(slot, turn_keys(slot)) for slot in (2, 3)]
+        scores_up_to(1)
 
         before = None
-        waiting_keys = None
-        rel_sorted = None
         for n in range(UNITS):
             g, c = divmod(n, CHUNKS)
             prepare = g + 1 < GROUPS
             y_t = work.tile([P, PACK, CHUNK], F32, name="y_t")
             for t in range(PACK):
-                add_bias(n, t, score[t], y_t)
-                if n + 1 < UNITS:
-                    score[t] = scores(n + 1, t)
-                if t == 0 and before is not None:
-                    round_part(nc.vector.tensor_copy, before[0], before[1], CHUNK - CAST_ON_VECTOR, CHUNK)
+                index = PACK * n + t
+                add_bias(n, t, score[index], y_t)
+                if n == 0 and t < 2:
+                    quantize_keys(*waiting.pop(0))
+                scores_up_to(index + SCORE_BANKS if index > 0 else 2)
+                if t == 0 and n > 0:
+                    round_part(nc.vector.tensor_copy, before[0], before[1], before[2], CHUNK)
+                    store_y(n - 1, before[0], 0, 2)
+                    if prepare and c > 0:
+                        turn_rel(g + 1, rel_sorted, c - 1, nc.scalar.copy)
+                if t == 1 and n > 0:
+                    if waiting:
+                        quantize_keys(*waiting.pop(0))
+                    store_y(n - 1, before[0], 2, 2)
+                if t == 1 and n == 0:
+                    waiting.append((PACK, turn_keys(PACK)))
+                if t == 2 and n == 1:
+                    quantize_keys(*waiting.pop(0))
+                if t == 1 + (n == 0) and n + 5 < SLOTS:
+                    waiting.append((n + 5, turn_keys(n + 5)))
                 if t > 0:
                     relu_gain(n, t - 1, y_t)
-                if t == 1 and waiting_keys is not None:
-                    quantize_keys(*waiting_keys)
-                    waiting_keys = None
             relu_gain(n, PACK - 1, y_t)
-            if before is not None:
+            if n > 0:
                 quantize_y(n - 1, before[1])
-            y_bf = work.tile([P, CHUNK, PACK], BF16, name="y_bf", align_bytes=64)
-            if n + 1 < UNITS:
-                round_part(nc.scalar.copy, y_t, y_bf, 0, CHUNK - CAST_ON_VECTOR)
-            if prepare and c < 2:
-                waiting_keys = (g + 1, c, turn_keys(g + 1, c, nc.scalar.copy))
-            if prepare and c == 1:
+            if prepare and c == 0:
                 rel_sorted = sort_rel(g + 1)
-            if prepare and c == 2:
-                turn_rel(g + 1, rel_sorted, nc.scalar.copy)
-            store_y(n, turn_y(y_t), 2 if n + 1 < UNITS else 1)
-            before = (y_t, y_bf)
+            y_bf = work.tile([P, CHUNK, PACK], BF16, name="y_bf", align_bytes=64)
+            split = CHUNK - (CAST_ON_VECTOR_PREPARING if prepare else CAST_ON_VECTOR_LAST)
+            if n + 1 < UNITS:
+                round_part(nc.scalar.copy, y_t, y_bf, 0, split)
+            before = (y_t, y_bf, split)
         round_part(nc.vector.tensor_copy, before[0], before[1], 0, CHUNK)
-        quantize_y(UNITS - 1, before[1])
+        for s in range(SUBS):
+            store_y(UNITS - 1, before[0], s, 1)
+            if s == 1:
+                quantize_y(UNITS - 1, before[1])

@@ -22,13 +22,11 @@ GROUPS = LK // GROUP
 PASSES = D // GROUP
 CHUNK = 512
 CHUNKS = TOKENS // CHUNK
-UNITS = GROUPS * CHUNKS
-SUBS = CHUNK // P
-CAST_ON_VECTOR_PREPARING = 176
-CAST_ON_VECTOR_LAST = 96
+UNITS = [(g, CHUNK * c, CHUNK) for g in range(GROUPS) for c in range(CHUNKS)][:-1]
+UNITS = UNITS + [(GROUPS - 1, TOKENS - CHUNK, LQ), (GROUPS - 1, TOKENS - LQ, LQ)]
 SLOTS = GROUPS * PACK
-SCORE_BANKS = 3
-TURN_BANKS = 5
+SCORE_BANKS = 4
+TURN_BANKS = 4
 LENGTH = LK / 512
 
 ROW_LEN = 720
@@ -94,8 +92,7 @@ def tile_relu_relative_scores_g6_kernel(tc, x_words, x_scales, keys, rel_table, 
                 )
             return rel_sorted
 
-        def turn_rel(g, rel_sorted, b, copy):
-            bank = turn_bank()
+        def turn_rel(g, rel_sorted, b, copy, bank):
             count = 4 if b < 2 else 2
             for w in range(count):
                 word = 4 * b + w
@@ -126,71 +123,84 @@ def tile_relu_relative_scores_g6_kernel(tc, x_words, x_scales, keys, rel_table, 
         score = []
 
         def scores_up_to(last):
-            for index in range(len(score), min(last + 1, UNITS * PACK)):
+            for index in range(len(score), min(last + 1, len(UNITS) * PACK)):
                 n, t = divmod(index, PACK)
-                g, c = divmod(n, CHUNKS)
+                g, first, width = UNITS[n]
+                c, inside = divmod(first, CHUNK)
                 slot = PACK * g + t
-                bank = psum.tile([P, CHUNK], F32, name="score", tag="score%d" % (index % SCORE_BANKS))
+                bank = psum.tile([P, width], F32, name="score", tag="score%d" % (index % SCORE_BANKS))
                 for k in range(PASSES):
                     nc.tensor.matmul_mx(
                         out=bank[:],
                         lhsT=key_codes[slot][:, P * k : P * (k + 1)].bitcast(FP8X4),
                         lhsT_scale=key_scale[slot][:, P * k : P * (k + 1)],
-                        rhs=x_codes[c][:, k, :].bitcast(FP8X4),
-                        rhs_scale=x_scale[4 * k : P, CHUNK * c : CHUNK * (c + 1)],
+                        rhs=x_codes[c][:, k, inside : inside + width].bitcast(FP8X4),
+                        rhs_scale=x_scale[4 * k : P, first : first + width],
                         start=(k == 0),
                         stop=(k == PASSES - 1),
                     )
                 score.append(bank)
 
-        def add_bias(n, t, bank, y_t):
-            g, c = divmod(n, CHUNKS)
-            window = bias[g][:].bitcast(BF16)[:, 2 * c : 2 * c + 2, t : t + LQ]
+        def add_bias(n, t, y_t):
+            g, first, width = UNITS[n]
+            window = bias[g][:].bitcast(BF16)[:, first // LQ : (first + width) // LQ, t : t + LQ]
             nc.vector.tensor_tensor(
-                out=y_t[:, t, :].rearrange("p (h i) -> p h i", h=2),
-                in0=bank[:].rearrange("p (h i) -> p h i", h=2),
+                out=y_t[:, t, :].rearrange("p (h i) -> p h i", i=LQ),
+                in0=score[PACK * n + t][:].rearrange("p (h i) -> p h i", i=LQ),
                 in1=window[:, :, ::-1],
                 op=ALU.add,
             )
 
         def relu_gain(n, t, y_t):
-            g = n // CHUNKS
+            g = UNITS[n][0]
             nc.vector.tensor_scalar(
                 out=y_t[:, t, :], in0=y_t[:, t, :], scalar1=0.0, scalar2=gain[:, g, t : t + 1], op0=ALU.max, op1=ALU.mult
             )
 
         def round_part(copy, y_t, y_bf, first, last):
             copy(
-                out=y_bf[:, first:last, :].rearrange("p (c i) t -> p c t i", i=4),
-                in_=y_t[:, :, first:last].rearrange("p t (c i) -> p c t i", i=4),
+                out=y_bf[:, first:last, :].rearrange("p (c i) t -> p c t i", i=2),
+                in_=y_t[:, :, first:last].rearrange("p t (c i) -> p c t i", i=2),
+            )
+
+        def round_on_gpsimd(y_t, y_bf, first, last):
+            nc.gpsimd.tensor_scalar(
+                out=y_bf[:, first:last, :],
+                in0=y_t[:, :, first:last].rearrange("p t n -> p n t"),
+                scalar1=1.0,
+                scalar2=0.0,
+                op0=ALU.mult,
+                op1=ALU.add,
             )
 
         def quantize_y(n, y_bf):
-            g, c = divmod(n, CHUNKS)
-            y_codes = work.tile([P, CHUNK], U32, name="y_codes", align_bytes=64)
+            g, first, width = UNITS[n]
+            y_codes = work.tile([P, width], U32, name="y_codes", align_bytes=64)
             nc.vector.quantize_mx(
                 out=y_codes[:].bitcast(FP8X4),
-                scales=y_scale[g][:, CHUNK * c : CHUNK * (c + 1)],
+                scales=y_scale[g][:, first : first + width],
                 in_=y_bf[:].rearrange("p n t -> p (n t)"),
             )
-            dst = out_1[g, :, CHUNK * c : CHUNK * (c + 1), :].rearrange("p n t -> p (n t)")
+            dst = out_1[g, :, first : first + width, :].rearrange("p n t -> p (n t)")
             nc.sync.dma_start(out=dst.bitcast(I32), in_=y_codes[:].bitcast(I32))
-            if c == CHUNKS - 1:
+            if first + width == TOKENS:
                 for q in range(4):
                     nc.sync.dma_start(
                         out=out_2[g, 4 * q : 4 * q + 4, :].bitcast(I32),
                         in_=y_scale[g][32 * q : 32 * q + 4, :].bitcast(I32),
                     )
 
-        def store_y(n, y_t, first, count):
-            g, c = divmod(n, CHUNKS)
+        def store_y(n, y_t, half):
+            g, first, width = UNITS[n]
+            count = width // (2 * P)
             y_out = work.tile([P, count, P, PACK], F32, name="y_out", tag="y_out", bufs=4)
             for s in range(count):
                 bank = turn_bank()
+                column = P * (count * half + s)
                 for t in range(PACK):
-                    nc.tensor.transpose(bank[:, t, :], y_t[:, t, P * (first + s) : P * (first + s + 1)], ident[:])
+                    nc.tensor.transpose(bank[:, t, :], y_t[:, t, column : column + P], ident[:])
                 nc.scalar.copy(out=y_out[:, s], in_=bank[:].rearrange("q t p -> q p t"))
-            row = CHUNK * c + P * first
+            row = first + P * count * half
             dst = y_rows[row : row + P * count, GROUP * g : GROUP * (g + 1)]
             nc.sync.dma_start(
                 out=dst.rearrange("(s q) j -> q s j", q=P),
@@ -208,77 +218,80 @@ def tile_relu_relative_scores_g6_kernel(tc, x_words, x_scales, keys, rel_table, 
         make_identity(nc, ident[:])
         load_keys(0)
         load_rel(0)
+        load_keys(1)
         load_x(0)
+        load_keys(2)
         for q in range(4):
             load_x_scale(q)
-        for slot in range(1, PACK):
-            load_keys(slot)
+        load_keys(3)
+        load_x(1)
         nc.sync.dma_start(out=gain_raw[:], in_=key_gain.rearrange("(g p t) -> p g t", p=P, t=PACK))
         load_keys(4)
-        load_x(1)
         load_keys(5)
-        load_rel(1)
-        load_keys(6)
         load_x(2)
-        load_keys(7)
+        load_keys(6)
+        load_rel(1)
         load_x(3)
-        for slot in range(2 * PACK, SLOTS):
+        for slot in range(7, SLOTS):
             load_keys(slot)
         load_rel(2)
 
         rel_sorted = sort_rel(0)
         grouped = turn_keys(0)
-        turn_rel(0, rel_sorted, 0, nc.scalar.copy)
-        quantize_keys(0, grouped)
-        turn_rel(0, rel_sorted, 1, nc.vector.tensor_copy)
-        turn_rel(0, rel_sorted, 2, nc.vector.tensor_copy)
+        for b, copy in enumerate((nc.scalar.copy, nc.vector.tensor_copy, nc.vector.tensor_copy)):
+            bank = psum.tile([P, PACK, P], F32, name="rel_bank", tag="score%d" % (b + 1))
+            turn_rel(0, rel_sorted, b, copy, bank)
+            if b == 0:
+                quantize_keys(0, grouped)
         grouped = turn_keys(1)
+        waiting = [(2, turn_keys(2))]
         scores_up_to(0)
-        nc.vector.tensor_scalar(out=gain[:], in0=gain_raw[:], scalar1=1.0 / LENGTH, scalar2=None, op0=ALU.mult)
+        waiting.append((3, turn_keys(3)))
         quantize_keys(1, grouped)
-        waiting = [(slot, turn_keys(slot)) for slot in (2, 3)]
         scores_up_to(1)
 
-        before = None
-        for n in range(UNITS):
-            g, c = divmod(n, CHUNKS)
+        y_t, y_bf = None, None
+        for n, (g, first, width) in enumerate(UNITS):
+            c = first // CHUNK
             prepare = g + 1 < GROUPS
-            y_t = work.tile([P, PACK, CHUNK], F32, name="y_t")
+            y_t_before, y_bf_before = y_t, y_bf
+            y_t = work.tile([P, PACK, width], F32, name="y_t")
+            y_bf = work.tile([P, width, PACK], BF16, name="y_bf", align_bytes=64)
+            if prepare and c > 1:
+                for b in ((0, 2), (1,))[c - 2]:
+                    turn_rel(g + 1, rel_sorted, b, nc.scalar.copy, turn_bank())
+            if n > 0:
+                store_y(n - 1, y_t_before, 0)
+            ready = waiting
+            waiting = []
             for t in range(PACK):
                 index = PACK * n + t
-                add_bias(n, t, score[index], y_t)
+                add_bias(n, t, y_t)
                 if n == 0 and t < 2:
-                    quantize_keys(*waiting.pop(0))
+                    quantize_keys(*ready.pop(0))
+                if t == PACK - 1:
+                    for slot, grouped in ready:
+                        quantize_keys(slot, grouped)
                 scores_up_to(index + SCORE_BANKS if index > 0 else 2)
-                if t == 0 and n > 0:
-                    round_part(nc.vector.tensor_copy, before[0], before[1], before[2], CHUNK)
-                    store_y(n - 1, before[0], 0, 2)
-                    if prepare and c > 0:
-                        turn_rel(g + 1, rel_sorted, c - 1, nc.scalar.copy)
-                if t == 1 and n > 0:
-                    if waiting:
-                        quantize_keys(*waiting.pop(0))
-                    store_y(n - 1, before[0], 2, 2)
-                if t == 1 and n == 0:
+                if t == 0 and n == 0:
                     waiting.append((PACK, turn_keys(PACK)))
-                if t == 2 and n == 1:
-                    quantize_keys(*waiting.pop(0))
-                if t == 1 + (n == 0) and n + 5 < SLOTS:
+                if t == 1 and n > 0:
+                    store_y(n - 1, y_t_before, 1)
+                if t == 1 and n + 5 < SLOTS:
                     waiting.append((n + 5, turn_keys(n + 5)))
-                if t > 0:
-                    relu_gain(n, t - 1, y_t)
-            relu_gain(n, PACK - 1, y_t)
             if n > 0:
-                quantize_y(n - 1, before[1])
-            if prepare and c == 0:
+                quantize_y(n - 1, y_bf_before)
+            if prepare and c == 1:
                 rel_sorted = sort_rel(g + 1)
-            y_bf = work.tile([P, CHUNK, PACK], BF16, name="y_bf", align_bytes=64)
-            split = CHUNK - (CAST_ON_VECTOR_PREPARING if prepare else CAST_ON_VECTOR_LAST)
-            if n + 1 < UNITS:
-                round_part(nc.scalar.copy, y_t, y_bf, 0, split)
-            before = (y_t, y_bf, split)
-        round_part(nc.vector.tensor_copy, before[0], before[1], 0, CHUNK)
-        for s in range(SUBS):
-            store_y(UNITS - 1, before[0], s, 1)
-            if s == 1:
-                quantize_y(UNITS - 1, before[1])
+            if n == 0:
+                nc.vector.tensor_scalar(out=gain[:], in0=gain_raw[:], scalar1=1.0 / LENGTH, scalar2=None, op0=ALU.mult)
+            for t in range(PACK):
+                relu_gain(n, t, y_t)
+            if n + 1 < len(UNITS):
+                round_on_gpsimd(y_t, y_bf, width // 2, width)
+                round_part(nc.scalar.copy, y_t, y_bf, 0, width // 2)
+        last = len(UNITS) - 1
+        round_part(nc.vector.tensor_copy, y_t, y_bf, 0, width)
+        store_y(last, y_t, 0)
+        quantize_y(last, y_bf)
+        store_y(last, y_t, 1)

from contextlib import ExitStack

import concourse.mybir as mybir
from concourse.masks import make_identity

H, LQ, LK, D = 8, 256, 1536, 1024
TOKENS = H * LQ
FLOPS = 2 * TOKENS * LK * D

F32 = mybir.dt.float32
BF16 = mybir.dt.bfloat16
I32 = mybir.dt.int32
U32 = mybir.dt.uint32
U8 = mybir.dt.uint8
FP8X4 = mybir.dt.float8_e4m3fn_x4
ALU = mybir.AluOpType

P = 128
PACK = 4
GROUP = P * PACK
GROUPS = LK // GROUP
PASSES = D // GROUP
CHUNK = 512
CHUNKS = TOKENS // CHUNK
UNITS = [(g, CHUNK * c, CHUNK) for g in range(GROUPS) for c in range(CHUNKS)][:-1]
UNITS = UNITS + [(GROUPS - 1, TOKENS - CHUNK, LQ), (GROUPS - 1, TOKENS - LQ, LQ)]
SLOTS = GROUPS * PACK
SCORE_BANKS = 4
TURN_BANKS = 4
LENGTH = LK / 512

ROW_LEN = 720
ROW_WORDS = ROW_LEN // 2
SORT_LEN = 132
HEAD_WORDS = 132


def tile_relu_relative_scores_g6_kernel(tc, x_words, x_scales, keys, rel_table, key_gain, out_0, out_1, out_2):
    nc = tc.nc
    y_rows = out_0.rearrange("h i j -> (h i) j")

    with ExitStack() as ctx:
        keep = ctx.enter_context(tc.tile_pool(name="keep", bufs=1))
        work = ctx.enter_context(tc.tile_pool(name="work", bufs=3))
        psum = ctx.enter_context(tc.psum_pool(name="psum", bufs=1))
        ctx.enter_context(tc.manual_schedule())

        turn_count = []

        def turn_bank():
            bank = psum.tile([P, PACK, P], F32, name="turn", tag="turn%d" % (len(turn_count) % TURN_BANKS))
            turn_count.append(0)
            return bank

        ident = keep.tile([P, P], F32)
        x_scale = keep.tile([P, TOKENS], U8, align_bytes=64)
        gain_raw = keep.tile([P, GROUPS, PACK], BF16)
        gain = keep.tile([P, GROUPS, PACK], F32)
        rel_rows = [keep.tile([P, ROW_LEN], BF16, name="rel_rows%d" % g) for g in range(GROUPS)]
        bias = [keep.tile([P, H, HEAD_WORDS], F32, name="bias%d" % g) for g in range(GROUPS)]
        x_codes = [keep.tile([P, PASSES, CHUNK], U32, name="x_codes%d" % c, align_bytes=64) for c in range(CHUNKS)]
        key_raw = [keep.tile([P, D], BF16, name="key_raw%d" % s) for s in range(SLOTS)]
        key_codes = [keep.tile([P, PASSES * P], U32, name="key_codes%d" % s, align_bytes=64) for s in range(SLOTS)]
        key_scale = [keep.tile([P, PASSES * P], U8, name="key_scale%d" % s, align_bytes=64) for s in range(SLOTS)]
        y_scale = [keep.tile([P, TOKENS], U8, name="y_scale%d" % g, align_bytes=64) for g in range(GROUPS)]

        def load_rel(g):
            for r in range(4):
                first = GROUP * g + 16 * r
                width = min(ROW_LEN, LQ + LK - 1 - first)
                nc.sync.dma_start(
                    out=rel_rows[g][r:P:4, 0:width],
                    in_=rel_table[:, first : first + width].unsqueeze(0).broadcast_to([4, H, width]),
                )

        def load_keys(slot):
            g, t = divmod(slot, PACK)
            nc.sync.dma_start(out=key_raw[slot][:], in_=keys[GROUP * g + t : GROUP * (g + 1) : PACK, :])

        def load_x(c):
            src = x_words[:, :, CHUNK * c : CHUNK * (c + 1), :].rearrange("g p n t -> p g (n t)")
            nc.sync.dma_start(out=x_codes[c][:].bitcast(I32), in_=src.bitcast(I32))

        def sort_rel(g):
            rel_sorted = work.tile([P, 2, SORT_LEN], F32, name="rel_sorted", bufs=2)
            words = rel_rows[g][:].bitcast(F32)
            for q in range(4):
                rows = slice(32 * q, 32 * (q + 1))
                nc.vector.tensor_copy(
                    out=rel_sorted[rows, :, :],
                    in_=words[rows, 32 * q : 32 * q + 2 * SORT_LEN].rearrange("p (m u) -> p u m", u=2),
                )
            return rel_sorted

        def turn_rel(g, rel_sorted, b, copy, bank):
            count = 4 if b < 2 else 2
            for w in range(count):
                word = 4 * b + w
                nc.tensor.transpose(bank[:, w, :], rel_sorted[:, word % 2, word // 2 : word // 2 + P], ident[:])
            if b < 2:
                dst = bias[g][:, :, 0:P].rearrange("p h (q r w) -> p q h r w", q=4, r=4)[:, :, :, :, 4 * b : 4 * b + 4]
                copy(out=dst, in_=bank[:].rearrange("p w (q h r) -> p q h r w", q=4, r=4))
            else:
                copy(out=bias[g][:, :, P : P + 2], in_=bank[:, 0:2, 99:P:4].rearrange("p w h -> p h w"))

        def turn_keys(slot):
            grouped = work.tile([P, PASSES, P, 2], F32, name="grouped", bufs=4, align_bytes=64)
            words = key_raw[slot][:].bitcast(F32)
            bank = turn_bank()
            for k in range(PASSES):
                for u in range(2):
                    nc.tensor.transpose(bank[:, 2 * k + u, :], words[:, 256 * k + u : 256 * (k + 1) : 2], ident[:])
            nc.scalar.copy(out=grouped[:], in_=bank[:].rearrange("p (k u) m -> p k m u", u=2))
            return grouped

        def quantize_keys(slot, grouped):
            nc.vector.quantize_mx(
                out=key_codes[slot][:].bitcast(FP8X4),
                scales=key_scale[slot][:],
                in_=grouped[:].rearrange("p k m u -> p (k m u)").bitcast(BF16),
            )

        score = []

        def scores_up_to(last):
            for index in range(len(score), min(last + 1, len(UNITS) * PACK)):
                n, t = divmod(index, PACK)
                g, first, width = UNITS[n]
                c, inside = divmod(first, CHUNK)
                slot = PACK * g + t
                bank = psum.tile([P, width], F32, name="score", tag="score%d" % (index % SCORE_BANKS))
                for k in range(PASSES):
                    nc.tensor.matmul_mx(
                        out=bank[:],
                        lhsT=key_codes[slot][:, P * k : P * (k + 1)].bitcast(FP8X4),
                        lhsT_scale=key_scale[slot][:, P * k : P * (k + 1)],
                        rhs=x_codes[c][:, k, inside : inside + width].bitcast(FP8X4),
                        rhs_scale=x_scale[4 * k : P, first : first + width],
                        start=(k == 0),
                        stop=(k == PASSES - 1),
                    )
                score.append(bank)

        def add_bias(n, t, y_t):
            g, first, width = UNITS[n]
            window = bias[g][:].bitcast(BF16)[:, first // LQ : (first + width) // LQ, t : t + LQ]
            nc.vector.tensor_tensor(
                out=y_t[:, t, :].rearrange("p (h i) -> p h i", i=LQ),
                in0=score[PACK * n + t][:].rearrange("p (h i) -> p h i", i=LQ),
                in1=window[:, :, ::-1],
                op=ALU.add,
            )

        def relu_gain(n, t, y_t):
            g = UNITS[n][0]
            nc.vector.tensor_scalar(
                out=y_t[:, t, :], in0=y_t[:, t, :], scalar1=0.0, scalar2=gain[:, g, t : t + 1], op0=ALU.max, op1=ALU.mult
            )

        def round_part(copy, y_t, y_bf, first, last):
            copy(
                out=y_bf[:, first:last, :].rearrange("p (c i) t -> p c t i", i=2),
                in_=y_t[:, :, first:last].rearrange("p t (c i) -> p c t i", i=2),
            )

        def round_on_gpsimd(y_t, y_bf, first, last):
            nc.gpsimd.tensor_scalar(
                out=y_bf[:, first:last, :],
                in0=y_t[:, :, first:last].rearrange("p t n -> p n t"),
                scalar1=1.0,
                scalar2=0.0,
                op0=ALU.mult,
                op1=ALU.add,
            )

        def quantize_y(n, y_bf):
            g, first, width = UNITS[n]
            y_codes = work.tile([P, width], U32, name="y_codes", align_bytes=64)
            nc.vector.quantize_mx(
                out=y_codes[:].bitcast(FP8X4),
                scales=y_scale[g][:, first : first + width],
                in_=y_bf[:].rearrange("p n t -> p (n t)"),
            )
            dst = out_1[g, :, first : first + width, :].rearrange("p n t -> p (n t)")
            nc.sync.dma_start(out=dst.bitcast(I32), in_=y_codes[:].bitcast(I32))
            if first + width == TOKENS:
                for q in range(4):
                    nc.sync.dma_start(
                        out=out_2[g, 4 * q : 4 * q + 4, :].bitcast(I32),
                        in_=y_scale[g][32 * q : 32 * q + 4, :].bitcast(I32),
                    )

        def store_y(n, y_t, half):
            g, first, width = UNITS[n]
            count = width // (2 * P)
            y_out = work.tile([P, count, P, PACK], F32, name="y_out", tag="y_out", bufs=4)
            for s in range(count):
                bank = turn_bank()
                column = P * (count * half + s)
                for t in range(PACK):
                    nc.tensor.transpose(bank[:, t, :], y_t[:, t, column : column + P], ident[:])
                nc.scalar.copy(out=y_out[:, s], in_=bank[:].rearrange("q t p -> q p t"))
            row = first + P * count * half
            dst = y_rows[row : row + P * count, GROUP * g : GROUP * (g + 1)]
            nc.sync.dma_start(
                out=dst.rearrange("(s q) j -> q s j", q=P),
                in_=y_out[:].rearrange("q s p t -> q s (p t)"),
            )

        def load_x_scale(q):
            nc.sync.dma_start(
                out=x_scale[32 * q : 32 * q + 4 * PASSES, :].bitcast(I32),
                in_=x_scales[:, 4 * q : 4 * q + 4, :].bitcast(I32),
            )

        nc.vector.memset(x_scale[:].bitcast(U32), 0)
        nc.vector.memset(rel_rows[GROUPS - 1][:, ROW_LEN - 2 : ROW_LEN], 0.0)
        make_identity(nc, ident[:])
        load_keys(0)
        load_rel(0)
        load_keys(1)
        load_x(0)
        load_keys(2)
        for q in range(4):
            load_x_scale(q)
        load_keys(3)
        load_x(1)
        nc.sync.dma_start(out=gain_raw[:], in_=key_gain.rearrange("(g p t) -> p g t", p=P, t=PACK))
        load_keys(4)
        load_keys(5)
        load_x(2)
        load_keys(6)
        load_rel(1)
        load_x(3)
        for slot in range(7, SLOTS):
            load_keys(slot)
        load_rel(2)

        rel_sorted = sort_rel(0)
        grouped = turn_keys(0)
        for b, copy in enumerate((nc.scalar.copy, nc.vector.tensor_copy, nc.vector.tensor_copy)):
            bank = psum.tile([P, PACK, P], F32, name="rel_bank", tag="score%d" % (b + 1))
            turn_rel(0, rel_sorted, b, copy, bank)
            if b == 0:
                quantize_keys(0, grouped)
        grouped = turn_keys(1)
        waiting = [(2, turn_keys(2))]
        scores_up_to(0)
        waiting.append((3, turn_keys(3)))
        quantize_keys(1, grouped)
        scores_up_to(1)

        y_t, y_bf = None, None
        for n, (g, first, width) in enumerate(UNITS):
            c = first // CHUNK
            prepare = g + 1 < GROUPS
            y_t_before, y_bf_before = y_t, y_bf
            y_t = work.tile([P, PACK, width], F32, name="y_t")
            y_bf = work.tile([P, width, PACK], BF16, name="y_bf", align_bytes=64)
            if prepare and c > 1:
                for b in ((0, 2), (1,))[c - 2]:
                    turn_rel(g + 1, rel_sorted, b, nc.scalar.copy, turn_bank())
            if n > 0:
                store_y(n - 1, y_t_before, 0)
            ready = waiting
            waiting = []
            for t in range(PACK):
                index = PACK * n + t
                add_bias(n, t, y_t)
                if n == 0 and t < 2:
                    quantize_keys(*ready.pop(0))
                if t == PACK - 1:
                    for slot, grouped in ready:
                        quantize_keys(slot, grouped)
                scores_up_to(index + SCORE_BANKS if index > 0 else 2)
                if t == 0 and n == 0:
                    waiting.append((PACK, turn_keys(PACK)))
                if t == 1 and n > 0:
                    store_y(n - 1, y_t_before, 1)
                if t == 1 and n + 5 < SLOTS:
                    waiting.append((n + 5, turn_keys(n + 5)))
            if n > 0:
                quantize_y(n - 1, y_bf_before)
            if prepare and c == 1:
                rel_sorted = sort_rel(g + 1)
            if n == 0:
                nc.vector.tensor_scalar(out=gain[:], in0=gain_raw[:], scalar1=1.0 / LENGTH, scalar2=None, op0=ALU.mult)
            for t in range(PACK):
                relu_gain(n, t, y_t)
            if n + 1 < len(UNITS):
                round_on_gpsimd(y_t, y_bf, width // 2, width)
                round_part(nc.scalar.copy, y_t, y_bf, 0, width // 2)
        last = len(UNITS) - 1
        round_part(nc.vector.tensor_copy, y_t, y_bf, 0, width)
        store_y(last, y_t, 0)
        quantize_y(last, y_bf)
        store_y(last, y_t, 1)
